import numpy as np
import ml_dtypes


def mxq(x, axis, fmt="e4m3"):
    dtype, down = {"e4m3": (ml_dtypes.float8_e4m3fn, 7), "e5m2": (ml_dtypes.float8_e5m2, 14)}[fmt]
    v = np.moveaxis(np.asarray(x, np.float32).astype(ml_dtypes.bfloat16).astype(np.float64), axis, -1)
    blocks = v.reshape(v.shape[:-1] + (-1, 32))
    amax = np.abs(blocks).max(-1, keepdims=True)
    byte = np.maximum(np.where(amax > 0, np.frexp(amax)[1] - 1 + 127, 0) - down, 1)
    scale = np.exp2(byte - 127.0)
    codes = (blocks / scale).astype(np.float32).astype(dtype).astype(np.float64)
    return np.moveaxis((codes * scale).reshape(v.shape), -1, axis)


WIDE = False


def mx_kscale(k):
    if not WIDE:
        return np.ones(k)
    levels = np.array([10, -10, 5, -5, 0])
    if k % 512:
        return np.exp2(np.random.permutation(np.resize(levels, k // 32))).repeat(32)
    a = np.empty((k // 512, 16))
    for p in range(k // 512):
        a[p, :8] = np.random.permutation(np.resize(levels, 8))
        for g in range(8):
            far = levels[np.abs(levels - a[p, g]) >= 10]
            a[p, g + 8] = far[np.random.randint(len(far))]
    return np.exp2(a.ravel()).repeat(32)


def f64(x):
    return np.asarray(x).astype(np.float64)


def striped(idx):
    return np.tile(np.asarray(idx).reshape(-1, 16).T, (8, 1)).astype(np.uint16)


def unstriped(offs):
    return offs[:16].T.reshape(-1).astype(np.int64)


E2M1 = np.array([0.0, 0.5, 1.0, 1.5, 2.0, 3.0, 4.0, 6.0, -0.0, -0.5, -1.0, -1.5, -2.0, -3.0, -4.0, -6.0])


def pack_weight(w, fmt):
    k, n = w.shape
    w = f64(np.asarray(w, np.float32).astype(ml_dtypes.bfloat16)).reshape(k // 32, 32, n)
    amax = np.abs(w).max(1)
    if fmt == "e4m3":
        byte = np.frexp(amax)[1] - 1 + 127 - 7
    else:
        mant, ex = np.frexp(amax / 6.0)
        byte = np.where(mant > 0.5, ex, ex - 1) + 127
    byte = np.clip(np.where(amax > 0, byte, 1), 1, 254)
    scaled = (w * np.exp2(127.0 - byte)[:, None, :]).reshape(k, n).astype(np.float32)
    by_word = np.ascontiguousarray(scaled.reshape(k // 512, 128, 4, n).transpose(0, 1, 3, 2))
    if fmt == "e4m3":
        words = by_word.astype(ml_dtypes.float8_e4m3fn).view(np.uint8)
    else:
        c = by_word.astype(ml_dtypes.float4_e2m1fn).view(np.uint8) & 0xF
        words = (c[..., 0::2] | (c[..., 1::2] << 4)).reshape(k // 512, 128, 2 * n)
    return np.ascontiguousarray(words), np.ascontiguousarray(byte.astype(np.uint8).reshape(k // 512, 16, n))


def unpack_weight(words, scales, fmt):
    g, _, n = scales.shape
    words = np.ascontiguousarray(words).reshape(g, 128, n, -1)
    if fmt == "e4m3":
        vals = words.view(ml_dtypes.float8_e4m3fn).astype(np.float64)
    else:
        nib = np.empty((g, 128, n, 4), np.uint8)
        nib[..., 0::2] = words & 0xF
        nib[..., 1::2] = words >> 4
        vals = E2M1[nib]
    vals = vals * np.repeat(np.exp2(scales.astype(np.float64) - 127.0), 8, axis=1)[..., None]
    return vals.transpose(0, 1, 3, 2).reshape(g * 512, n)


def bf(x):
    return np.asarray(x, np.float32).astype(ml_dtypes.bfloat16)


def planes(Y):
    r, m = Y.shape
    b = f64(bf(Y)).reshape(r // 32, 32, m)
    amax = np.abs(b).max(1)
    byte = np.clip(np.where(amax > 0, np.frexp(amax)[1] - 1 + 127 - 7, 1), 1, 254)
    codes = (b * np.exp2(127.0 - byte)[:, None, :]).reshape(r, m).astype(np.float32).astype(ml_dtypes.float8_e4m3fn).view(np.uint8)
    words = codes.reshape(r // 512, 128, 4, m).transpose(0, 1, 3, 2)
    return np.ascontiguousarray(words), np.ascontiguousarray(byte.astype(np.uint8).reshape(r // 512, 16, m))


K, T, J, N, R = 1024, 2048, 512, 512, 512


def setup_inputs():
    n = np.random.standard_normal
    idx = np.random.permutation(T)[:J]
    fk = mx_kscale(K)
    fr = mx_kscale(R)
    xqp = pack_weight(n((K, T)) / fk[:, None], "e2m1")
    wap = pack_weight(n((K, R)) * 1 / np.sqrt(K) * fk[:, None] * fr, "e4m3")
    wbp = pack_weight(n((K, R)) * 1 / np.sqrt(K) * fk[:, None] * fr, "e2m1")
    wdp = pack_weight(n((R, N)) * 1 / np.sqrt(R) / fr[:, None], "e4m3")
    return {
        "xq_words": xqp[0],
        "xq_scales": xqp[1],
        "wa_words": wap[0],
        "wa_scales": wap[1],
        "wb_words": wbp[0],
        "wb_scales": wbp[1],
        "wd_words": wdp[0],
        "wd_scales": wdp[1],
        "ga": (np.random.uniform(0.4, 1.2, (1, J))).astype(np.float32),
        "offs": striped(idx),
    }


def reference(xq_words, xq_scales, wa_words, wa_scales, wb_words, wb_scales, wd_words, wd_scales, ga, offs):
    idx = unstriped(offs)
    xqu = unpack_weight(xq_words, xq_scales, "e2m1")
    wau = unpack_weight(wa_words, wa_scales, "e4m3")
    wbu = unpack_weight(wb_words, wb_scales, "e2m1")
    wdu = unpack_weight(wd_words, wd_scales, "e4m3")
    xqidxg = xqu[:, idx]
    a = wau.T @ xqidxg
    b = wbu.T @ xqidxg
    hid = np.maximum(a, b)
    hidq = mxq(hid, 0, "e4m3")
    p = wdu.T @ hidq
    y = p * f64(ga)
    words, scales = planes(y)
    return y, words, scales

@@ -1,0 +1,199 @@
+from contextlib import ExitStack
+
+import concourse.mybir as mybir
+from concourse.masks import make_identity
+
+K, T, J, N, R = 1024, 2048, 512, 512, 512
+FLOPS = 2 * K * R * J * 2 + 2 * R * N * J
+
+F32 = mybir.dt.float32
+BF16 = mybir.dt.bfloat16
+I32 = mybir.dt.int32
+U32 = mybir.dt.uint32
+U16 = mybir.dt.uint16
+U8 = mybir.dt.uint8
+FP8X4 = mybir.dt.float8_e4m3fn_x4
+FP4X4 = mybir.dt.float4_e2m1fn_x4
+ALU = mybir.AluOpType
+
+P = 128
+PASSES = K // 512
+CH = 128
+NCH = J // CH
+HALF = 256
+
+
+def load_scales(queue, plane, scales, quadrants):
+    for q in quadrants:
+        queue.dma_start(
+            out=plane[32 * q : 32 * q + 4].bitcast(I32),
+            in_=scales[:, 4 * q : 4 * q + 4, :].rearrange("z r c -> r z c").bitcast(I32),
+        )
+
+
+def tile_list_expert_larger_half_pl_kernel(
+    tc, xq_words, xq_scales, wa_words, wa_scales, wb_words, wb_scales, wd_words, wd_scales, ga, offs, out_0, out_1, out_2
+):
+    nc = tc.nc
+    with ExitStack() as ctx:
+        keep = ctx.enter_context(tc.tile_pool(name="keep", bufs=1))
+        laid = ctx.enter_context(tc.tile_pool(name="laid", bufs=1))
+        psum = ctx.enter_context(tc.psum_pool(name="psum", bufs=1))
+
+        xs_at = 2048
+        xs = laid.tile([P, T], U8, name="xs", offset=xs_at, align_bytes=64)
+        was = keep.tile([P, PASSES, R], U8, name="was", align_bytes=64)
+        gs1 = keep.tile([P, J], U8, name="gs1", align_bytes=64)
+        nc.vector.memset(xs[:].bitcast(I32), 0)
+        nc.gpsimd.memset(was[:].rearrange("p z c -> p (z c)").bitcast(I32), 0)
+        nc.vector.memset(gs1[:].bitcast(I32), 0)
+
+        offsets = keep.tile([P, J // 16], U16, name="offsets")
+        nc.sync.dma_start(offsets[:], offs)
+        xw = [keep.tile([P, T], U16, name="xw%d" % z, tag="xw%d" % z, align_bytes=64) for z in range(PASSES)]
+        nc.sync.dma_start(out=xw[0][:].bitcast(I32), in_=xq_words[0].bitcast(I32))
+        for q in range(4):
+            nc.scalar.dma_start(
+                out=xs[32 * q : 32 * q + 8, :].bitcast(I32),
+                in_=xq_scales[:, 4 * q : 4 * q + 4, :].bitcast(I32),
+            )
+        wa = keep.tile([P, PASSES, R], I32, name="wa", align_bytes=64)
+        nc.sync.dma_start(out=wa[:], in_=wa_words.rearrange("z p c t -> p z (c t)").bitcast(I32))
+        nc.sync.dma_start(out=xw[1][:].bitcast(I32), in_=xq_words[1].bitcast(I32))
+        load_scales(nc.gpsimd, was, wa_scales, range(4))
+        ident = keep.tile([P, P], F32, name="ident")
+        make_identity(nc, ident[:])
+
+        gs0 = keep.tile([P, J], U8, name="gs0", align_bytes=64)
+        gs = [gs0, gs1]
+        nc.vector.tensor_copy(out=gs0[:], in_=xs[:].indirect(offsets[:]))
+        nc.sync.dma_start(out=gs1[0:64, :].bitcast(I32), in_=gs0[4:68, :].bitcast(I32))
+        for q in (2, 3):
+            nc.sync.dma_start(out=gs1[32 * q : 32 * q + 4, :].bitcast(I32), in_=gs0[32 * q + 4 : 32 * q + 8, :].bitcast(I32))
+        gw_all = laid.tile([P, PASSES * J], U16, name="gw_all", offset=64, align_bytes=64)
+        gw = [gw_all[:, z * J : (z + 1) * J] for z in range(PASSES)]
+        for z in range(PASSES):
+            for h in range(J // HALF):
+                cols = slice(h * HALF, (h + 1) * HALF)
+                part = offsets[:, h * HALF // 16 : (h + 1) * HALF // 16]
+                nc.vector.tensor_copy(out=gw[z][:, cols], in_=xw[z][:].indirect(part))
+
+        w2 = laid.tile([P, 8 * N], U8, name="w2", offset=xs_at + 64 + 1024 + 512, align_bytes=64)
+        wb = w2[:, : 4 * N].rearrange("p (z c) -> p z c", z=PASSES)
+        wd = w2[:, 4 * N :].bitcast(U32)
+        wbs = laid.tile([P, PASSES, R], U8, name="wbs", offset=xs_at + 64, align_bytes=64)
+        wds_t = laid.tile([P, N], U8, name="wds_t", offset=xs_at + 64 + 1024, align_bytes=64)
+        wds = wds_t[:]
+        nc.sync.dma_start(out=wb.bitcast(I32), in_=wb_words.rearrange("z p c -> p z c").bitcast(I32))
+        nc.gpsimd.memset(wbs[:].rearrange("p z c -> p (z c)").bitcast(I32), 0)
+        load_scales(nc.sync, wbs, wb_scales, range(4))
+        nc.gpsimd.memset(wds.bitcast(I32), 0)
+        nc.sync.dma_start(out=wd.bitcast(I32), in_=wd_words[0].rearrange("p c t -> p (c t)").bitcast(I32))
+        for q in range(4):
+            nc.sync.dma_start(out=wds[32 * q : 32 * q + 4, :].bitcast(I32), in_=wd_scales[0, 4 * q : 4 * q + 4, :].bitcast(I32))
+        ga_all = keep.tile([P, J], F32, name="ga_all", tag="xw0", align_bytes=64)
+        nc.sync.dma_start(out=ga_all[:], in_=ga[0].partition_broadcast(P))
+
+        wd_d = keep.tile([P, N], U32, name="wd_d", align_bytes=64)
+        nc.scalar.copy(
+            out=wd_d[:].rearrange("p (t c i) -> p c t i", t=4, i=4),
+            in_=wd.rearrange("p (c i t) -> p c t i", t=4, i=4),
+        )
+        wds_d = keep.tile([P, N], U8, name="wds_d", align_bytes=64)
+        nc.vector.tensor_copy(
+            out=wds_d[:].rearrange("p (t m) -> p m t", t=4),
+            in_=wds.rearrange("p (m t) -> p m t", t=4),
+        )
+
+        yq = keep.tile([P, J], U32, name="yq", align_bytes=64)
+        ys = keep.tile([P, J], U8, name="ys", align_bytes=64)
+        out_rows = out_0.rearrange("(p t) j -> p t j", t=4)
+
+        a_ps, b_ps, hid = {}, {}, {}
+
+        def first(c, z):
+            cols = slice(c * CH, (c + 1) * CH)
+            if z == 0:
+                a_ps[c] = psum.tile([P, R], F32, name="a_ps%d" % c, tag="a%d" % c)
+            nc.tensor.matmul_mx(
+                out=a_ps[c][:], lhsT=gw[z][:, cols].bitcast(FP4X4), lhsT_scale=gs[z][:, cols],
+                rhs=wa[:, z, :].bitcast(FP8X4), rhs_scale=was[:, z, :], start=(z == 0), stop=(z == PASSES - 1),
+            )
+
+        def second(c, z):
+            cols = slice(c * CH, (c + 1) * CH)
+            if z == 0:
+                b_ps[c] = psum.tile([P, R], F32, name="b_ps%d" % c, tag="b%d" % c)
+            nc.tensor.matmul_mx(
+                out=b_ps[c][:], lhsT=gw[z][:, cols].bitcast(FP4X4), lhsT_scale=gs[z][:, cols],
+                rhs=wb[:, z, :].bitcast(FP4X4), rhs_scale=wbs[:, z, :], start=(z == 0), stop=(z == PASSES - 1),
+            )
+
+        def stage1(c):
+            for z in range(PASSES):
+                first(c, z)
+            for z in range(PASSES):
+                second(c, z)
+
+        def larger(c):
+            a_sb = keep.tile([P, R], F32, name="a_sb%d" % c)
+            nc.scalar.copy(
+                out=a_sb[:].rearrange("j (u p e) -> j u p e", u=2, e=2),
+                in_=a_ps[c][:].rearrange("j (p u e) -> j u p e", u=2, e=2),
+            )
+            hid[c] = keep.tile([P, R], BF16, name="hid%d" % c, align_bytes=64)
+            nc.vector.tensor_tensor(
+                out=hid[c][:].rearrange("j (u p e) -> j u p e", u=2, e=2),
+                in0=b_ps[c][:].rearrange("j (p u e) -> j u p e", u=2, e=2),
+                in1=a_sb[:].rearrange("j (u p e) -> j u p e", u=2, e=2),
+                op=ALU.max,
+            )
+
+        def stage2(c):
+            cols = slice(c * CH, (c + 1) * CH)
+            pairs = hid[c][:].bitcast(F32)
+            t_ps = psum.tile([P, 2, CH], F32, name="t_ps%d" % c, tag="a%d" % c)
+            for u in range(2):
+                nc.tensor.transpose(t_ps[:, u, :], pairs[:, u * P : (u + 1) * P], ident[:])
+            woven = keep.tile([P, CH * 4], BF16, name="woven%d" % c, align_bytes=64)
+            nc.scalar.copy(
+                out=woven[:].bitcast(F32).rearrange("p (j u) -> p j u", u=2),
+                in_=t_ps[:].rearrange("p u j -> p j u"),
+            )
+            hq = keep.tile([P, CH], U32, name="hq%d" % c, align_bytes=64)
+            hs = keep.tile([P, CH], U8, name="hs%d" % c, align_bytes=64)
+            nc.vector.quantize_mx(out=hq[:].bitcast(FP8X4), scales=hs[:], in_=woven[:])
+            p_ps = psum.tile([P, 4, CH], F32, name="p_ps%d" % c, tag="b%d" % c)
+            for t in range(4):
+                nc.tensor.matmul_mx(
+                    out=p_ps[:, t, :],
+                    lhsT=wd_d[:, t * P : (t + 1) * P].bitcast(FP8X4),
+                    lhsT_scale=wds_d[:, t * P : (t + 1) * P],
+                    rhs=hq[:].bitcast(FP8X4),
+                    rhs_scale=hs[:],
+                    start=True,
+                    stop=True,
+                )
+            y = keep.tile([P, 4, CH], F32, name="y%d" % c)
+            nc.vector.tensor_tensor(
+                out=y[:], in0=p_ps[:], in1=ga_all[:, cols].unsqueeze(1).to_broadcast([P, 4, CH]), op=ALU.mult
+            )
+            nc.sync.dma_start(out=out_rows[:, :, cols], in_=y[:])
+            yb = keep.tile([P, CH * 4], BF16, name="yb%d" % c, align_bytes=64)
+            nc.scalar.copy(
+                out=yb[:].rearrange("p (g i t) -> p g t i", t=4, i=4),
+                in_=y[:].rearrange("p t (g i) -> p g t i", i=4),
+            )
+            nc.vector.quantize_mx(out=yq[:, cols].bitcast(FP8X4), scales=ys[:, cols], in_=yb[:])
+
+        for c in range(NCH + 1):
+            if c < NCH:
+                stage1(c)
+                larger(c)
+            if c > 0:
+                stage2(c - 1)
+
+        nc.sync.dma_start(out=out_1[0].rearrange("p c t -> p (c t)").bitcast(I32), in_=yq[:].bitcast(I32))
+        for q in range(4):
+            queue = nc.scalar if q % 2 else nc.sync
+            queue.dma_start(out=out_2[0, 4 * q : 4 * q + 4, :].bitcast(I32), in_=ys[32 * q : 32 * q + 4, :].bitcast(I32))

@@ -1,7 +1,6 @@
 from contextlib import ExitStack
 
 import concourse.mybir as mybir
-from concourse.masks import make_identity
 
 K, T, J, N, R = 1024, 2048, 512, 512, 512
 FLOPS = 2 * K * R * J * 2 + 2 * R * N * J
@@ -37,62 +36,57 @@ def tile_list_expert_larger_half_pl_kernel(
     nc = tc.nc
     with ExitStack() as ctx:
         keep = ctx.enter_context(tc.tile_pool(name="keep", bufs=1))
-        laid = ctx.enter_context(tc.tile_pool(name="laid", bufs=1))
         psum = ctx.enter_context(tc.psum_pool(name="psum", bufs=1))
 
-        xs_at = 2048
-        xs = laid.tile([P, T], U8, name="xs", offset=xs_at, align_bytes=64)
+        xs = keep.tile([P, PASSES, T], U8, name="xs", align_bytes=64)
         was = keep.tile([P, PASSES, R], U8, name="was", align_bytes=64)
-        gs1 = keep.tile([P, J], U8, name="gs1", align_bytes=64)
-        nc.vector.memset(xs[:].bitcast(I32), 0)
-        nc.gpsimd.memset(was[:].rearrange("p z c -> p (z c)").bitcast(I32), 0)
-        nc.vector.memset(gs1[:].bitcast(I32), 0)
+        wbs = keep.tile([P, PASSES, R], U8, name="wbs", align_bytes=64)
+        wds_t = keep.tile([P, 1, N], U8, name="wds_t", align_bytes=64)
+        for plane in (xs, was, wbs, wds_t):
+            nc.vector.memset(plane[:].rearrange("p z c -> p (z c)").bitcast(I32), 0)
+        wds = wds_t[:, 0, :]
 
         offsets = keep.tile([P, J // 16], U16, name="offsets")
         nc.sync.dma_start(offsets[:], offs)
-        xw = [keep.tile([P, T], U16, name="xw%d" % z, tag="xw%d" % z, align_bytes=64) for z in range(PASSES)]
+        xw = [keep.tile([P, T], U16, name="xw%d" % z, align_bytes=64) for z in range(PASSES)]
         nc.sync.dma_start(out=xw[0][:].bitcast(I32), in_=xq_words[0].bitcast(I32))
-        for q in range(4):
-            nc.scalar.dma_start(
-                out=xs[32 * q : 32 * q + 8, :].bitcast(I32),
-                in_=xq_scales[:, 4 * q : 4 * q + 4, :].bitcast(I32),
-            )
+        ga_col = keep.tile([P, 4], F32, name="ga_col")
+        nc.sync.dma_start(out=ga_col[:], in_=ga.rearrange("o (p c) -> (o p) c", c=4))
+        load_scales(nc.scalar, xs, xq_scales, range(4))
+        nc.gpsimd.dma_start(out=xw[1][:].bitcast(I32), in_=xq_words[1].bitcast(I32))
         wa = keep.tile([P, PASSES, R], I32, name="wa", align_bytes=64)
-        nc.sync.dma_start(out=wa[:], in_=wa_words.rearrange("z p c t -> p z (c t)").bitcast(I32))
-        nc.sync.dma_start(out=xw[1][:].bitcast(I32), in_=xq_words[1].bitcast(I32))
-        load_scales(nc.gpsimd, was, wa_scales, range(4))
-        ident = keep.tile([P, P], F32, name="ident")
-        make_identity(nc, ident[:])
+        nc.gpsimd.dma_start(out=wa[:], in_=wa_words.rearrange("z p c t -> p z (c t)").bitcast(I32))
+        wb = keep.tile([P, PASSES, 2 * R], U8, name="wb", align_bytes=64)
+        nc.gpsimd.dma_start(out=wb[:].bitcast(I32), in_=wb_words.rearrange("z p c -> p z c").bitcast(I32))
+        load_scales(nc.sync, was, wa_scales, range(4))
+        load_scales(nc.sync, wbs, wb_scales, range(4))
+        load_scales(nc.sync, wds_t, wd_scales, range(4))
 
-        gs0 = keep.tile([P, J], U8, name="gs0", align_bytes=64)
-        gs = [gs0, gs1]
-        nc.vector.tensor_copy(out=gs0[:], in_=xs[:].indirect(offsets[:]))
-        nc.sync.dma_start(out=gs1[0:64, :].bitcast(I32), in_=gs0[4:68, :].bitcast(I32))
-        for q in (2, 3):
-            nc.sync.dma_start(out=gs1[32 * q : 32 * q + 4, :].bitcast(I32), in_=gs0[32 * q + 4 : 32 * q + 8, :].bitcast(I32))
-        gw_all = laid.tile([P, PASSES * J], U16, name="gw_all", offset=64, align_bytes=64)
-        gw = [gw_all[:, z * J : (z + 1) * J] for z in range(PASSES)]
-        for z in range(PASSES):
-            for h in range(J // HALF):
-                cols = slice(h * HALF, (h + 1) * HALF)
-                part = offsets[:, h * HALF // 16 : (h + 1) * HALF // 16]
+        zeros = keep.tile([P, P], F32, name="zeros", tag="wd", align_bytes=64)
+        nc.gpsimd.memset(zeros[:], 0.0)
+        ident = keep.tile([P, P], F32, name="ident")
+        nc.gpsimd.affine_select(
+            out=ident[:], in_=zeros[:], compare_op=ALU.not_equal, fill=1.0, base=0,
+            pattern=[[-1, P]], channel_multiplier=1,
+        )
+        wd_t = keep.tile([P, N], U32, name="wd_t", tag="wd", align_bytes=64)
+        wd = wd_t[:]
+        nc.sync.dma_start(out=wd.bitcast(I32), in_=wd_words[0].rearrange("p c t -> p (c t)").bitcast(I32))
+
+        gw = [keep.tile([P, J], U16, name="gw%d" % z, align_bytes=64) for z in range(PASSES)]
+        gs = [keep.tile([P, J], U8, name="gs%d" % z, align_bytes=64) for z in range(PASSES)]
+        for h in range(J // HALF):
+            cols = slice(h * HALF, (h + 1) * HALF)
+            part = offsets[:, h * HALF // 16 : (h + 1) * HALF // 16]
+            for z in range(PASSES):
+                nc.vector.tensor_copy(out=gs[z][:, cols], in_=xs[:, z, :].indirect(part))
                 nc.vector.tensor_copy(out=gw[z][:, cols], in_=xw[z][:].indirect(part))
 
-        w2 = laid.tile([P, 8 * N], U8, name="w2", offset=xs_at + 64 + 1024 + 512, align_bytes=64)
-        wb = w2[:, : 4 * N].rearrange("p (z c) -> p z c", z=PASSES)
-        wd = w2[:, 4 * N :].bitcast(U32)
-        wbs = laid.tile([P, PASSES, R], U8, name="wbs", offset=xs_at + 64, align_bytes=64)
-        wds_t = laid.tile([P, N], U8, name="wds_t", offset=xs_at + 64 + 1024, align_bytes=64)
-        wds = wds_t[:]
-        nc.sync.dma_start(out=wb.bitcast(I32), in_=wb_words.rearrange("z p c -> p z c").bitcast(I32))
-        nc.gpsimd.memset(wbs[:].rearrange("p z c -> p (z c)").bitcast(I32), 0)
-        load_scales(nc.sync, wbs, wb_scales, range(4))
-        nc.gpsimd.memset(wds.bitcast(I32), 0)
-        nc.sync.dma_start(out=wd.bitcast(I32), in_=wd_words[0].rearrange("p c t -> p (c t)").bitcast(I32))
-        for q in range(4):
-            nc.sync.dma_start(out=wds[32 * q : 32 * q + 4, :].bitcast(I32), in_=wd_scales[0, 4 * q : 4 * q + 4, :].bitcast(I32))
-        ga_all = keep.tile([P, J], F32, name="ga_all", tag="xw0", align_bytes=64)
-        nc.sync.dma_start(out=ga_all[:], in_=ga[0].partition_broadcast(P))
+        ga_ps = psum.tile([P, 4, P], F32, name="ga_ps", tag="b3")
+        for c in range(4):
+            nc.tensor.transpose(ga_ps[:, c, :], ga_col[:, c : c + 1].to_broadcast([P, P]), ident[:])
+        ga_all = keep.tile([P, J], F32, name="ga_all")
+        nc.scalar.copy(out=ga_all[:].rearrange("p (m c) -> p m c", c=4), in_=ga_ps[:].rearrange("p c m -> p m c"))
 
         wd_d = keep.tile([P, N], U32, name="wd_d", align_bytes=64)
         nc.scalar.copy(
@@ -108,6 +102,8 @@ def tile_list_expert_larger_half_pl_kernel(
         yq = keep.tile([P, J], U32, name="yq", align_bytes=64)
         ys = keep.tile([P, J], U8, name="ys", align_bytes=64)
         out_rows = out_0.rearrange("(p t) j -> p t j", t=4)
+
+        out_words = out_1[0].rearrange("p c t -> p (c t)").bitcast(I32)
 
         a_ps, b_ps, hid = {}, {}, {}
 
@@ -185,15 +181,29 @@ def tile_list_expert_larger_half_pl_kernel(
                 in_=y[:].rearrange("p t (g i) -> p g t i", i=4),
             )
             nc.vector.quantize_mx(out=yq[:, cols].bitcast(FP8X4), scales=ys[:, cols], in_=yb[:])
+            if c % 2:
+                two = slice((c - 1) * CH, (c + 1) * CH)
+                nc.sync.dma_start(out=out_words[:, two], in_=yq[:, two].bitcast(I32))
 
-        for c in range(NCH + 1):
-            if c < NCH:
-                stage1(c)
-                larger(c)
-            if c > 0:
-                stage2(c - 1)
+        first(0, 0)
+        first(1, 0)
+        first(0, 1)
+        second(0, 0)
+        second(0, 1)
+        larger(0)
+        first(1, 1)
+        second(1, 0)
+        second(1, 1)
+        larger(1)
+        stage2(0)
+        stage1(2)
+        larger(2)
+        stage2(1)
+        stage1(3)
+        larger(3)
+        stage2(2)
+        stage2(3)
 
-        nc.sync.dma_start(out=out_1[0].rearrange("p c t -> p (c t)").bitcast(I32), in_=yq[:].bitcast(I32))
         for q in range(4):
             queue = nc.scalar if q % 2 else nc.sync
             queue.dma_start(out=out_2[0, 4 * q : 4 * q + 4, :].bitcast(I32), in_=ys[32 * q : 32 * q + 4, :].bitcast(I32))

@@ -52,7 +52,7 @@ def tile_list_expert_larger_half_pl_kernel(
         nc.sync.dma_start(out=xw[0][:].bitcast(I32), in_=xq_words[0].bitcast(I32))
         ga_col = keep.tile([P, 4], F32, name="ga_col")
         nc.sync.dma_start(out=ga_col[:], in_=ga.rearrange("o (p c) -> (o p) c", c=4))
-        load_scales(nc.scalar, xs, xq_scales, range(4))
+        load_scales(nc.sync, xs, xq_scales, range(4))
         nc.gpsimd.dma_start(out=xw[1][:].bitcast(I32), in_=xq_words[1].bitcast(I32))
         wa = keep.tile([P, PASSES, R], I32, name="wa", align_bytes=64)
         nc.gpsimd.dma_start(out=wa[:], in_=wa_words.rearrange("z p c t -> p z (c t)").bitcast(I32))
@@ -78,9 +78,10 @@ def tile_list_expert_larger_half_pl_kernel(
         for h in range(J // HALF):
             cols = slice(h * HALF, (h + 1) * HALF)
             part = offsets[:, h * HALF // 16 : (h + 1) * HALF // 16]
+            nc.vector.tensor_copy(out=gw[0][:, cols], in_=xw[0][:].indirect(part))
             for z in range(PASSES):
                 nc.vector.tensor_copy(out=gs[z][:, cols], in_=xs[:, z, :].indirect(part))
-                nc.vector.tensor_copy(out=gw[z][:, cols], in_=xw[z][:].indirect(part))
+            nc.vector.tensor_copy(out=gw[1][:, cols], in_=xw[1][:].indirect(part))
 
         ga_ps = psum.tile([P, 4, P], F32, name="ga_ps", tag="b3")
         for c in range(4):
@@ -176,25 +177,22 @@ def tile_list_expert_larger_half_pl_kernel(
             )
             nc.sync.dma_start(out=out_rows[:, :, cols], in_=y[:])
             yb = keep.tile([P, CH * 4], BF16, name="yb%d" % c, align_bytes=64)
-            nc.scalar.copy(
+            cast = nc.vector.tensor_copy if c == NCH - 1 else nc.scalar.copy
+            cast(
                 out=yb[:].rearrange("p (g i t) -> p g t i", t=4, i=4),
                 in_=y[:].rearrange("p t (g i) -> p g t i", i=4),
             )
             nc.vector.quantize_mx(out=yq[:, cols].bitcast(FP8X4), scales=ys[:, cols], in_=yb[:])
-            if c % 2:
-                two = slice((c - 1) * CH, (c + 1) * CH)
-                nc.sync.dma_start(out=out_words[:, two], in_=yq[:, two].bitcast(I32))
+            nc.sync.dma_start(out=out_words[:, cols], in_=yq[:, cols].bitcast(I32))
 
-        first(0, 0)
-        first(1, 0)
-        first(0, 1)
-        second(0, 0)
-        second(0, 1)
-        larger(0)
-        first(1, 1)
-        second(1, 0)
-        second(1, 1)
-        larger(1)
+        for c in range(2):
+            first(c, 0)
+        for c in range(2):
+            second(c, 0)
+        for c in range(2):
+            first(c, 1)
+            second(c, 1)
+            larger(c)
         stage2(0)
         stage1(2)
         larger(2)

@@ -1,6 +1,7 @@
 from contextlib import ExitStack
 
 import concourse.mybir as mybir
+from concourse.masks import make_identity
 
 K, T, J, N, R = 1024, 2048, 512, 512, 512
 FLOPS = 2 * K * R * J * 2 + 2 * R * N * J
@@ -38,49 +39,47 @@ def tile_list_expert_larger_half_pl_kernel(
         keep = ctx.enter_context(tc.tile_pool(name="keep", bufs=1))
         psum = ctx.enter_context(tc.psum_pool(name="psum", bufs=1))
 
-        xs = keep.tile([P, PASSES, T], U8, name="xs", align_bytes=64)
+        ident = keep.tile([P, P], F32, name="ident")
+        make_identity(nc, ident[:])
+
+        xs = keep.tile([P, PASSES, T], U8, name="xs", tag="xs", align_bytes=64)
         was = keep.tile([P, PASSES, R], U8, name="was", align_bytes=64)
         wbs = keep.tile([P, PASSES, R], U8, name="wbs", align_bytes=64)
-        wds_t = keep.tile([P, 1, N], U8, name="wds_t", align_bytes=64)
-        for plane in (xs, was, wbs, wds_t):
+        for plane in (xs, was, wbs):
             nc.vector.memset(plane[:].rearrange("p z c -> p (z c)").bitcast(I32), 0)
-        wds = wds_t[:, 0, :]
 
         offsets = keep.tile([P, J // 16], U16, name="offsets")
         nc.sync.dma_start(offsets[:], offs)
-        xw = [keep.tile([P, T], U16, name="xw%d" % z, align_bytes=64) for z in range(PASSES)]
+        xw = [keep.tile([P, T], U16, name="xw%d" % z, tag="xw%d" % z, align_bytes=64) for z in range(PASSES)]
         nc.sync.dma_start(out=xw[0][:].bitcast(I32), in_=xq_words[0].bitcast(I32))
         ga_col = keep.tile([P, 4], F32, name="ga_col")
         nc.sync.dma_start(out=ga_col[:], in_=ga.rearrange("o (p c) -> (o p) c", c=4))
         load_scales(nc.sync, xs, xq_scales, range(4))
-        nc.gpsimd.dma_start(out=xw[1][:].bitcast(I32), in_=xq_words[1].bitcast(I32))
         wa = keep.tile([P, PASSES, R], I32, name="wa", align_bytes=64)
         nc.gpsimd.dma_start(out=wa[:], in_=wa_words.rearrange("z p c t -> p z (c t)").bitcast(I32))
-        wb = keep.tile([P, PASSES, 2 * R], U8, name="wb", align_bytes=64)
-        nc.gpsimd.dma_start(out=wb[:].bitcast(I32), in_=wb_words.rearrange("z p c -> p z c").bitcast(I32))
+        nc.gpsimd.dma_start(out=xw[1][:].bitcast(I32), in_=xq_words[1].bitcast(I32))
         load_scales(nc.sync, was, wa_scales, range(4))
         load_scales(nc.sync, wbs, wb_scales, range(4))
-        load_scales(nc.sync, wds_t, wd_scales, range(4))
-
-        zeros = keep.tile([P, P], F32, name="zeros", tag="wd", align_bytes=64)
-        nc.gpsimd.memset(zeros[:], 0.0)
-        ident = keep.tile([P, P], F32, name="ident")
-        nc.gpsimd.affine_select(
-            out=ident[:], in_=zeros[:], compare_op=ALU.not_equal, fill=1.0, base=0,
-            pattern=[[-1, P]], channel_multiplier=1,
-        )
-        wd_t = keep.tile([P, N], U32, name="wd_t", tag="wd", align_bytes=64)
-        wd = wd_t[:]
-        nc.sync.dma_start(out=wd.bitcast(I32), in_=wd_words[0].rearrange("p c t -> p (c t)").bitcast(I32))
 
         gw = [keep.tile([P, J], U16, name="gw%d" % z, align_bytes=64) for z in range(PASSES)]
         gs = [keep.tile([P, J], U8, name="gs%d" % z, align_bytes=64) for z in range(PASSES)]
+        nc.vector.tensor_copy(out=gw[0][:], in_=xw[0][:].indirect(offsets[:]))
+        wb = keep.tile([P, PASSES, 2 * R], U8, name="wb", tag="xw0", align_bytes=64)
+        nc.sync.dma_start(out=wb[:].bitcast(I32), in_=wb_words.rearrange("z p c -> p z c").bitcast(I32))
+        for z in range(PASSES):
+            nc.vector.tensor_copy(out=gs[z][:], in_=xs[:, z, :].indirect(offsets[:]))
+        w2 = keep.tile([P, 5 * N], U8, name="w2", tag="xs", align_bytes=64)
+        wd = w2[:, : 4 * N].bitcast(U32)
+        wds = w2[:, 4 * N :]
+        nc.gpsimd.memset(wds.bitcast(I32), 0)
+        nc.sync.dma_start(out=wd.bitcast(I32), in_=wd_words[0].rearrange("p c t -> p (c t)").bitcast(I32))
+        for q in range(4):
+            nc.sync.dma_start(
+                out=wds[32 * q : 32 * q + 4, :].bitcast(I32), in_=wd_scales[0, 4 * q : 4 * q + 4, :].bitcast(I32)
+            )
         for h in range(J // HALF):
             cols = slice(h * HALF, (h + 1) * HALF)
             part = offsets[:, h * HALF // 16 : (h + 1) * HALF // 16]
-            nc.vector.tensor_copy(out=gw[0][:, cols], in_=xw[0][:].indirect(part))
-            for z in range(PASSES):
-                nc.vector.tensor_copy(out=gs[z][:, cols], in_=xs[:, z, :].indirect(part))
             nc.vector.tensor_copy(out=gw[1][:, cols], in_=xw[1][:].indirect(part))
 
         ga_ps = psum.tile([P, 4, P], F32, name="ga_ps", tag="b3")
@@ -88,17 +87,6 @@ def tile_list_expert_larger_half_pl_kernel(
             nc.tensor.transpose(ga_ps[:, c, :], ga_col[:, c : c + 1].to_broadcast([P, P]), ident[:])
         ga_all = keep.tile([P, J], F32, name="ga_all")
         nc.scalar.copy(out=ga_all[:].rearrange("p (m c) -> p m c", c=4), in_=ga_ps[:].rearrange("p c m -> p m c"))
-
-        wd_d = keep.tile([P, N], U32, name="wd_d", align_bytes=64)
-        nc.scalar.copy(
-            out=wd_d[:].rearrange("p (t c i) -> p c t i", t=4, i=4),
-            in_=wd.rearrange("p (c i t) -> p c t i", t=4, i=4),
-        )
-        wds_d = keep.tile([P, N], U8, name="wds_d", align_bytes=64)
-        nc.vector.tensor_copy(
-            out=wds_d[:].rearrange("p (t m) -> p m t", t=4),
-            in_=wds.rearrange("p (m t) -> p m t", t=4),
-        )
 
         yq = keep.tile([P, J], U32, name="yq", align_bytes=64)
         ys = keep.tile([P, J], U8, name="ys", align_bytes=64)
@@ -126,14 +114,8 @@ def tile_list_expert_larger_half_pl_kernel(
                 rhs=wb[:, z, :].bitcast(FP4X4), rhs_scale=wbs[:, z, :], start=(z == 0), stop=(z == PASSES - 1),
             )
 
-        def stage1(c):
-            for z in range(PASSES):
-                first(c, z)
-            for z in range(PASSES):
-                second(c, z)
-
         def larger(c):
-            a_sb = keep.tile([P, R], F32, name="a_sb%d" % c)
+            a_sb = keep.tile([P, R], F32, name="a_sb%d" % c, tag="a_sb%d" % c, align_bytes=64)
             nc.scalar.copy(
                 out=a_sb[:].rearrange("j (u p e) -> j u p e", u=2, e=2),
                 in_=a_ps[c][:].rearrange("j (p u e) -> j u p e", u=2, e=2),
@@ -145,6 +127,18 @@ def tile_list_expert_larger_half_pl_kernel(
                 in1=a_sb[:].rearrange("j (u p e) -> j u p e", u=2, e=2),
                 op=ALU.max,
             )
+
+        def deal_wd():
+            dealt = keep.tile([P, 5 * N], U8, name="dealt", tag="a_sb0", align_bytes=64)
+            words, scales = dealt[:, : 4 * N].bitcast(U32), dealt[:, 4 * N :]
+            nc.vector.tensor_copy(
+                out=scales.rearrange("p (t m) -> p m t", t=4), in_=wds.rearrange("p (m t) -> p m t", t=4)
+            )
+            nc.scalar.copy(
+                out=words.rearrange("p (t c i) -> p c t i", t=4, i=4),
+                in_=wd.rearrange("p (c i t) -> p c t i", t=4, i=4),
+            )
+            return words, scales
 
         def stage2(c):
             cols = slice(c * CH, (c + 1) * CH)
@@ -185,22 +179,19 @@ def tile_list_expert_larger_half_pl_kernel(
             nc.vector.quantize_mx(out=yq[:, cols].bitcast(FP8X4), scales=ys[:, cols], in_=yb[:])
             nc.sync.dma_start(out=out_words[:, cols], in_=yq[:, cols].bitcast(I32))
 
-        for c in range(2):
+        for c in range(NCH):
             first(c, 0)
-        for c in range(2):
+        for c in range(NCH):
             second(c, 0)
-        for c in range(2):
-            first(c, 1)
-            second(c, 1)
-            larger(c)
-        stage2(0)
-        stage1(2)
-        larger(2)
-        stage2(1)
-        stage1(3)
-        larger(3)
-        stage2(2)
-        stage2(3)
+        for c in range(NCH + 1):
+            if c < NCH:
+                first(c, 1)
+                second(c, 1)
+                larger(c)
+            if c == 0:
+                wd_d, wds_d = deal_wd()
+            if c > 0:
+                stage2(c - 1)
 
         for q in range(4):
             queue = nc.scalar if q % 2 else nc.sync

from contextlib import ExitStack

import concourse.mybir as mybir
from concourse.masks import make_identity

K, T, J, N, R = 1024, 2048, 512, 512, 512
FLOPS = 2 * K * R * J * 2 + 2 * R * N * J

F32 = mybir.dt.float32
BF16 = mybir.dt.bfloat16
I32 = mybir.dt.int32
U32 = mybir.dt.uint32
U16 = mybir.dt.uint16
U8 = mybir.dt.uint8
FP8X4 = mybir.dt.float8_e4m3fn_x4
FP4X4 = mybir.dt.float4_e2m1fn_x4
ALU = mybir.AluOpType

P = 128
PASSES = K // 512
CH = 128
NCH = J // CH
HALF = 256


def load_scales(queue, plane, scales, quadrants):
    for q in quadrants:
        queue.dma_start(
            out=plane[32 * q : 32 * q + 4].bitcast(I32),
            in_=scales[:, 4 * q : 4 * q + 4, :].rearrange("z r c -> r z c").bitcast(I32),
        )


def tile_list_expert_larger_half_pl_kernel(
    tc, xq_words, xq_scales, wa_words, wa_scales, wb_words, wb_scales, wd_words, wd_scales, ga, offs, out_0, out_1, out_2
):
    nc = tc.nc
    with ExitStack() as ctx:
        keep = ctx.enter_context(tc.tile_pool(name="keep", bufs=1))
        psum = ctx.enter_context(tc.psum_pool(name="psum", bufs=1))

        ident = keep.tile([P, P], F32, name="ident")
        make_identity(nc, ident[:])

        xs = keep.tile([P, PASSES, T], U8, name="xs", tag="xs", align_bytes=64)
        was = keep.tile([P, PASSES, R], U8, name="was", align_bytes=64)
        wbs = keep.tile([P, PASSES, R], U8, name="wbs", align_bytes=64)
        for plane in (xs, was, wbs):
            nc.vector.memset(plane[:].rearrange("p z c -> p (z c)").bitcast(I32), 0)

        offsets = keep.tile([P, J // 16], U16, name="offsets")
        nc.sync.dma_start(offsets[:], offs)
        xw = [keep.tile([P, T], U16, name="xw%d" % z, tag="xw%d" % z, align_bytes=64) for z in range(PASSES)]
        nc.sync.dma_start(out=xw[0][:].bitcast(I32), in_=xq_words[0].bitcast(I32))
        ga_col = keep.tile([P, 4], F32, name="ga_col")
        nc.sync.dma_start(out=ga_col[:], in_=ga.rearrange("o (p c) -> (o p) c", c=4))
        load_scales(nc.sync, xs, xq_scales, range(4))
        wa = keep.tile([P, PASSES, R], I32, name="wa", align_bytes=64)
        nc.gpsimd.dma_start(out=wa[:], in_=wa_words.rearrange("z p c t -> p z (c t)").bitcast(I32))
        nc.gpsimd.dma_start(out=xw[1][:].bitcast(I32), in_=xq_words[1].bitcast(I32))
        load_scales(nc.sync, was, wa_scales, range(4))
        load_scales(nc.sync, wbs, wb_scales, range(4))

        gw = [keep.tile([P, J], U16, name="gw%d" % z, align_bytes=64) for z in range(PASSES)]
        gs = [keep.tile([P, J], U8, name="gs%d" % z, align_bytes=64) for z in range(PASSES)]
        nc.vector.tensor_copy(out=gw[0][:], in_=xw[0][:].indirect(offsets[:]))
        wb = keep.tile([P, PASSES, 2 * R], U8, name="wb", tag="xw0", align_bytes=64)
        nc.sync.dma_start(out=wb[:].bitcast(I32), in_=wb_words.rearrange("z p c -> p z c").bitcast(I32))
        for z in range(PASSES):
            nc.vector.tensor_copy(out=gs[z][:], in_=xs[:, z, :].indirect(offsets[:]))
        w2 = keep.tile([P, 5 * N], U8, name="w2", tag="xs", align_bytes=64)
        wd = w2[:, : 4 * N].bitcast(U32)
        wds = w2[:, 4 * N :]
        nc.gpsimd.memset(wds.bitcast(I32), 0)
        nc.sync.dma_start(out=wd.bitcast(I32), in_=wd_words[0].rearrange("p c t -> p (c t)").bitcast(I32))
        for q in range(4):
            nc.sync.dma_start(
                out=wds[32 * q : 32 * q + 4, :].bitcast(I32), in_=wd_scales[0, 4 * q : 4 * q + 4, :].bitcast(I32)
            )
        for h in range(J // HALF):
            cols = slice(h * HALF, (h + 1) * HALF)
            part = offsets[:, h * HALF // 16 : (h + 1) * HALF // 16]
            nc.vector.tensor_copy(out=gw[1][:, cols], in_=xw[1][:].indirect(part))

        ga_ps = psum.tile([P, 4, P], F32, name="ga_ps", tag="b3")
        for c in range(4):
            nc.tensor.transpose(ga_ps[:, c, :], ga_col[:, c : c + 1].to_broadcast([P, P]), ident[:])
        ga_all = keep.tile([P, J], F32, name="ga_all")
        nc.scalar.copy(out=ga_all[:].rearrange("p (m c) -> p m c", c=4), in_=ga_ps[:].rearrange("p c m -> p m c"))

        yq = keep.tile([P, J], U32, name="yq", align_bytes=64)
        ys = keep.tile([P, J], U8, name="ys", align_bytes=64)
        out_rows = out_0.rearrange("(p t) j -> p t j", t=4)

        out_words = out_1[0].rearrange("p c t -> p (c t)").bitcast(I32)

        a_ps, b_ps, hid = {}, {}, {}

        def first(c, z):
            cols = slice(c * CH, (c + 1) * CH)
            if z == 0:
                a_ps[c] = psum.tile([P, R], F32, name="a_ps%d" % c, tag="a%d" % c)
            nc.tensor.matmul_mx(
                out=a_ps[c][:], lhsT=gw[z][:, cols].bitcast(FP4X4), lhsT_scale=gs[z][:, cols],
                rhs=wa[:, z, :].bitcast(FP8X4), rhs_scale=was[:, z, :], start=(z == 0), stop=(z == PASSES - 1),
            )

        def second(c, z):
            cols = slice(c * CH, (c + 1) * CH)
            if z == 0:
                b_ps[c] = psum.tile([P, R], F32, name="b_ps%d" % c, tag="b%d" % c)
            nc.tensor.matmul_mx(
                out=b_ps[c][:], lhsT=gw[z][:, cols].bitcast(FP4X4), lhsT_scale=gs[z][:, cols],
                rhs=wb[:, z, :].bitcast(FP4X4), rhs_scale=wbs[:, z, :], start=(z == 0), stop=(z == PASSES - 1),
            )

        def larger(c):
            a_sb = keep.tile([P, R], F32, name="a_sb%d" % c, tag="a_sb%d" % c, align_bytes=64)
            nc.scalar.copy(
                out=a_sb[:].rearrange("j (u p e) -> j u p e", u=2, e=2),
                in_=a_ps[c][:].rearrange("j (p u e) -> j u p e", u=2, e=2),
            )
            hid[c] = keep.tile([P, R], BF16, name="hid%d" % c, align_bytes=64)
            nc.vector.tensor_tensor(
                out=hid[c][:].rearrange("j (u p e) -> j u p e", u=2, e=2),
                in0=b_ps[c][:].rearrange("j (p u e) -> j u p e", u=2, e=2),
                in1=a_sb[:].rearrange("j (u p e) -> j u p e", u=2, e=2),
                op=ALU.max,
            )

        def deal_wd():
            dealt = keep.tile([P, 5 * N], U8, name="dealt", tag="a_sb0", align_bytes=64)
            words, scales = dealt[:, : 4 * N].bitcast(U32), dealt[:, 4 * N :]
            nc.vector.tensor_copy(
                out=scales.rearrange("p (t m) -> p m t", t=4), in_=wds.rearrange("p (m t) -> p m t", t=4)
            )
            nc.scalar.copy(
                out=words.rearrange("p (t c i) -> p c t i", t=4, i=4),
                in_=wd.rearrange("p (c i t) -> p c t i", t=4, i=4),
            )
            return words, scales

        def stage2(c):
            cols = slice(c * CH, (c + 1) * CH)
            pairs = hid[c][:].bitcast(F32)
            t_ps = psum.tile([P, 2, CH], F32, name="t_ps%d" % c, tag="a%d" % c)
            for u in range(2):
                nc.tensor.transpose(t_ps[:, u, :], pairs[:, u * P : (u + 1) * P], ident[:])
            woven = keep.tile([P, CH * 4], BF16, name="woven%d" % c, align_bytes=64)
            nc.scalar.copy(
                out=woven[:].bitcast(F32).rearrange("p (j u) -> p j u", u=2),
                in_=t_ps[:].rearrange("p u j -> p j u"),
            )
            hq = keep.tile([P, CH], U32, name="hq%d" % c, align_bytes=64)
            hs = keep.tile([P, CH], U8, name="hs%d" % c, align_bytes=64)
            nc.vector.quantize_mx(out=hq[:].bitcast(FP8X4), scales=hs[:], in_=woven[:])
            p_ps = psum.tile([P, 4, CH], F32, name="p_ps%d" % c, tag="b%d" % c)
            for t in range(4):
                nc.tensor.matmul_mx(
                    out=p_ps[:, t, :],
                    lhsT=wd_d[:, t * P : (t + 1) * P].bitcast(FP8X4),
                    lhsT_scale=wds_d[:, t * P : (t + 1) * P],
                    rhs=hq[:].bitcast(FP8X4),
                    rhs_scale=hs[:],
                    start=True,
                    stop=True,
                )
            y = keep.tile([P, 4, CH], F32, name="y%d" % c)
            nc.vector.tensor_tensor(
                out=y[:], in0=p_ps[:], in1=ga_all[:, cols].unsqueeze(1).to_broadcast([P, 4, CH]), op=ALU.mult
            )
            nc.sync.dma_start(out=out_rows[:, :, cols], in_=y[:])
            yb = keep.tile([P, CH * 4], BF16, name="yb%d" % c, align_bytes=64)
            cast = nc.vector.tensor_copy if c == NCH - 1 else nc.scalar.copy
            cast(
                out=yb[:].rearrange("p (g i t) -> p g t i", t=4, i=4),
                in_=y[:].rearrange("p t (g i) -> p g t i", i=4),
            )
            nc.vector.quantize_mx(out=yq[:, cols].bitcast(FP8X4), scales=ys[:, cols], in_=yb[:])
            nc.sync.dma_start(out=out_words[:, cols], in_=yq[:, cols].bitcast(I32))

        for c in range(NCH):
            first(c, 0)
        for c in range(NCH):
            second(c, 0)
        for c in range(NCH + 1):
            if c < NCH:
                first(c, 1)
                second(c, 1)
                larger(c)
            if c == 0:
                wd_d, wds_d = deal_wd()
            if c > 0:
                stage2(c - 1)

        for q in range(4):
            queue = nc.scalar if q % 2 else nc.sync
            queue.dma_start(out=out_2[0, 4 * q : 4 * q + 4, :].bitcast(I32), in_=ys[32 * q : 32 * q + 4, :].bitcast(I32))
